import numpy as np
import ml_dtypes


def mxq(x, axis, fmt="e4m3"):
    dtype, down = {"e4m3": (ml_dtypes.float8_e4m3fn, 7), "e5m2": (ml_dtypes.float8_e5m2, 14)}[fmt]
    v = np.moveaxis(np.asarray(x, np.float32).astype(ml_dtypes.bfloat16).astype(np.float64), axis, -1)
    blocks = v.reshape(v.shape[:-1] + (-1, 32))
    amax = np.abs(blocks).max(-1, keepdims=True)
    byte = np.maximum(np.where(amax > 0, np.frexp(amax)[1] - 1 + 127, 0) - down, 1)
    scale = np.exp2(byte - 127.0)
    codes = (blocks / scale).astype(np.float32).astype(dtype).astype(np.float64)
    return np.moveaxis((codes * scale).reshape(v.shape), -1, axis)


WIDE = False


def mx_kscale(k):
    if not WIDE:
        return np.ones(k)
    levels = np.array([10, -10, 5, -5, 0])
    if k % 512:
        return np.exp2(np.random.permutation(np.resize(levels, k // 32))).repeat(32)
    a = np.empty((k // 512, 16))
    for p in range(k // 512):
        a[p, :8] = np.random.permutation(np.resize(levels, 8))
        for g in range(8):
            far = levels[np.abs(levels - a[p, g]) >= 10]
            a[p, g + 8] = far[np.random.randint(len(far))]
    return np.exp2(a.ravel()).repeat(32)


BF16 = ml_dtypes.bfloat16


def bf(x):
    return np.asarray(x, np.float32).astype(BF16)


def f64(x):
    return np.asarray(x).astype(np.float64)


E2M1 = np.array([0.0, 0.5, 1.0, 1.5, 2.0, 3.0, 4.0, 6.0, -0.0, -0.5, -1.0, -1.5, -2.0, -3.0, -4.0, -6.0])


def pack_weight(w, fmt):
    k, n = w.shape
    w = f64(bf(w)).reshape(k // 32, 32, n)
    amax = np.abs(w).max(1)
    if fmt == "e4m3":
        byte = np.frexp(amax)[1] - 1 + 127 - 7
    else:
        mant, ex = np.frexp(amax / 6.0)
        byte = np.where(mant > 0.5, ex, ex - 1) + 127
    byte = np.clip(np.where(amax > 0, byte, 1), 1, 254)
    scaled = (w * np.exp2(127.0 - byte)[:, None, :]).reshape(k, n).astype(np.float32)
    by_word = np.ascontiguousarray(scaled.reshape(k // 512, 128, 4, n).transpose(0, 1, 3, 2))
    if fmt == "e4m3":
        words = by_word.astype(ml_dtypes.float8_e4m3fn).view(np.uint8)
    else:
        c = by_word.astype(ml_dtypes.float4_e2m1fn).view(np.uint8) & 0xF
        words = c[..., 0::2] | (c[..., 1::2] << 4)
    return np.ascontiguousarray(words), np.ascontiguousarray(byte.astype(np.uint8).reshape(k // 512, 16, n))


def unpack_weight(words, scales, fmt):
    g, p, n, _ = words.shape
    if fmt == "e4m3":
        vals = np.ascontiguousarray(words).view(ml_dtypes.float8_e4m3fn).astype(np.float64)
    else:
        nib = np.empty((g, p, n, 4), np.uint8)
        nib[..., 0::2] = words & 0xF
        nib[..., 1::2] = words >> 4
        vals = E2M1[nib]
    vals = vals * np.repeat(np.exp2(scales.astype(np.float64) - 127.0), 8, axis=1)[..., None]
    return vals.transpose(0, 1, 3, 2).reshape(g * 512, n)
def pack4(w):
    words, scales = pack_weight(w, "e2m1")
    return words.reshape(words.shape[0], 128, -1), scales


def unpack4(words, scales):
    return unpack_weight(words.reshape(words.shape[0], 128, -1, 2), scales, "e2m1")


def planes(Y):
    n, m = Y.shape
    b = f64(bf(Y)).reshape(n // 32, 32, m)
    amax = np.abs(b).max(1)
    byte = np.clip(np.where(amax > 0, np.frexp(amax)[1] - 1 + 127 - 7, 1), 1, 254)
    codes = (b * np.exp2(127.0 - byte)[:, None, :]).reshape(n, m).astype(np.float32).astype(ml_dtypes.float8_e4m3fn).view(np.uint8)
    words = codes.reshape(n // 512, 128, 4, m).transpose(0, 1, 3, 2)
    return np.ascontiguousarray(words), np.ascontiguousarray(byte.astype(np.uint8).reshape(n // 512, 16, m))


CELLS, MODES, DIMS = 1536, 512, 3


def setup_inputs():
    s = mx_kscale(CELLS)[:, None]
    tau = np.linspace(-1.0, 1.0, CELLS)[:, None]
    z = 1.5 * np.exp(0.35 * tau) * np.random.uniform(-1.0, 1.0, (CELLS, DIMS))
    dist = (tau - tau.T) ** 2
    for d in range(DIMS):
        dist = dist + (z[:, d:d + 1] - z[:, d:d + 1].T) ** 2
    kern = np.exp(-dist)
    kern = kern / kern.sum(axis=1).mean()
    h = 1.0 / kern.sum(axis=1, keepdims=True)
    r = 1.0 / (kern * h.T).sum(axis=1, keepdims=True)
    gain = np.exp(0.6 * np.random.randn(1, MODES))
    omega = np.random.uniform(0.5, 2.5, (2, MODES))
    phase = np.random.uniform(0.0, 2.0 * np.pi, (2, MODES))
    psi = 1.5 * gain * (np.cos(omega[:1] * tau + phase[:1]) + 0.5 * np.random.randn(CELLS, MODES))
    v = gain * (0.5 * np.random.randn(1, MODES) + np.cos(omega[1:] * z[:, :1] + phase[1:]) + 0.5 * np.random.randn(CELLS, MODES))
    w = np.exp(0.4 * np.random.randn(1, MODES) + 0.5 * np.random.randn(CELLS, MODES))
    x_words, x_scales = pack_weight(kern.T * s, "e4m3")
    w_words, w_scales = pack4(w * h / s)
    c_words, c_scales = pack_weight(w * v * h / s, "e4m3")
    return {"x_words": x_words, "x_scales": x_scales, "psi_h": bf(psi * h / s),
            "w_words": w_words, "w_scales": w_scales, "c_words": c_words, "c_scales": c_scales,
            "r": bf(r.reshape(CELLS)), "h": bf(h.reshape(CELLS))}

def reference(x_words, x_scales, psi_h, w_words, w_scales, c_words, c_scales, r, h):
    x = unpack_weight(x_words, x_scales, "e4m3")
    w = unpack4(w_words, w_scales)
    c = unpack_weight(c_words, c_scales, "e4m3")
    a = x.T @ mxq(f64(psi_h), 0, "e4m3")
    b = x.T @ w
    e = x.T @ c
    y = (a * f64(r)[:, None] + e / b) * f64(h)[:, None]
    Y = y
    words, scales = planes(Y)
    return y, words, scales

@@ -1,0 +1,305 @@
+from contextlib import ExitStack
+
+import concourse.mybir as mybir
+
+CELLS, MODES = 1536, 512
+FLOPS = 3 * 2 * CELLS * CELLS * MODES
+
+F32 = mybir.dt.float32
+BF16 = mybir.dt.bfloat16
+I32 = mybir.dt.int32
+U8 = mybir.dt.uint8
+FP8X4 = mybir.dt.float8_e4m3fn_x4
+FP4X4 = mybir.dt.float4_e2m1fn_x4
+ALU = mybir.AluOpType
+ACT = mybir.ActivationFunctionType
+
+P = 128
+PACK = 4
+K_PASS = P * PACK
+PASSES = CELLS // K_PASS
+GROUPS = CELLS // K_PASS
+QUADS = 4
+RUN = 4
+HALF = MODES // 2
+
+
+def tile_diffusion_map_step_k3_kernel(
+    tc, x_words, x_scales, psi_h, w_words, w_scales, c_words, c_scales, r, h, out_0, out_1, out_2
+):
+    nc = tc.nc
+    with ExitStack() as ctx:
+        keep = ctx.enter_context(tc.tile_pool(name="keep", bufs=1))
+        psum = ctx.enter_context(tc.psum_pool(name="psum", bufs=1))
+        ctx.enter_context(tc.manual_schedule())
+
+        def sbuf(name, shape, dtype, tag="", bufs=None):
+            return keep.tile(shape, dtype, name=name, tag=tag or name, bufs=bufs, align_bytes=256)
+
+        def live_rows(quad):
+            return slice(32 * quad, 32 * quad + 4)
+
+        def load_scales(queue, plane, scales, cols, quad):
+            rows = scales[:, 4 * quad : 4 * quad + 4, cols].rearrange("g r n -> r g n")
+            queue.dma_start(out=plane[live_rows(quad), :, :].bitcast(I32), in_=rows.bitcast(I32))
+
+        x_rows = x_words.rearrange("g p n t -> p g (n t)")
+        w_rows = w_words.rearrange("g p b -> p g b")
+        c_rows = c_words.rearrange("g p n t -> p g (n t)")
+
+        xs_first = sbuf("xs_first", [P, PASSES, K_PASS], U8)
+        xs_rest = sbuf("xs_rest", [P, PASSES, 2 * K_PASS], U8)
+        w_plane = sbuf("w_plane", [P, PASSES, MODES], U8)
+        c_plane = sbuf("c_plane", [P, PASSES, MODES], U8)
+        for plane in (xs_first, w_plane, c_plane, xs_rest):
+            nc.vector.memset(plane[:].bitcast(I32), 0)
+
+        x_first = [sbuf("x_first%d" % g, [P, K_PASS], I32) for g in range(PASSES)]
+        x_rest = [sbuf("x_rest%d" % i, [P, PASSES, K_PASS], I32) for i in range(GROUPS - 1)]
+        w_first = sbuf("w_first", [P, 2 * MODES], U8)
+        w_rest = sbuf("w_rest", [P, PASSES - 1, 2 * MODES], U8)
+        c_codes = sbuf("c_codes", [P, PASSES, MODES], I32)
+        psi_raw = [sbuf("psi_raw%d" % g, [P, PACK, MODES], BF16) for g in range(PASSES)]
+        r_col = sbuf("r_col", [P, GROUPS, PACK], BF16)
+        h_col = sbuf("h_col", [P, GROUPS, PACK], BF16)
+
+        def x_bytes(grp):
+            return slice(grp * K_PASS * PACK, (grp + 1) * K_PASS * PACK)
+
+        first_cols = slice(0, K_PASS)
+        all_modes = slice(0, MODES)
+        load_scales(nc.sync, xs_first, x_scales, first_cols, 0)
+        load_scales(nc.scalar, w_plane, w_scales, all_modes, 0)
+        nc.sync.dma_start(out=x_first[0][:], in_=x_rows[:, 0, x_bytes(0)].bitcast(I32))
+        nc.scalar.dma_start(out=w_first[:].bitcast(I32), in_=w_rows[:, 0, :].bitcast(I32))
+        load_scales(nc.sync, xs_first, x_scales, first_cols, 1)
+        load_scales(nc.scalar, w_plane, w_scales, all_modes, 1)
+        load_scales(nc.sync, xs_first, x_scales, first_cols, 2)
+        load_scales(nc.scalar, xs_first, x_scales, first_cols, 3)
+        load_scales(nc.sync, w_plane, w_scales, all_modes, 2)
+        load_scales(nc.scalar, w_plane, w_scales, all_modes, 3)
+        nc.sync.dma_start(out=x_first[1][:], in_=x_rows[:, 1, x_bytes(0)].bitcast(I32))
+        nc.sync.dma_start(out=w_rest[:].bitcast(I32), in_=w_rows[:, 1:, :].bitcast(I32))
+        nc.sync.dma_start(out=x_first[2][:], in_=x_rows[:, 2, x_bytes(0)].bitcast(I32))
+        for quad in range(QUADS):
+            load_scales(nc.sync, c_plane, c_scales, all_modes, quad)
+        nc.sync.dma_start(out=c_codes[:], in_=c_rows.bitcast(I32))
+
+        def load_psi(g):
+            rows = psi_h[g * K_PASS : (g + 1) * K_PASS, :]
+            nc.sync.dma_start(out=psi_raw[g][:], in_=rows.rearrange("(p j) f -> p j f", j=PACK))
+
+        load_psi(0)
+        for quad in range(QUADS):
+            load_scales(nc.sync, xs_rest, x_scales, slice(K_PASS, CELLS), quad)
+        nc.sync.dma_start(out=x_rest[0][:], in_=x_rows[:, :, x_bytes(1)].bitcast(I32))
+        nc.sync.dma_start(out=h_col[:], in_=h.rearrange("(g p t) -> p g t", p=P, t=PACK))
+        nc.sync.dma_start(out=r_col[:], in_=r.rearrange("(g p t) -> p g t", p=P, t=PACK))
+        load_psi(1)
+        load_psi(2)
+        nc.sync.dma_start(out=x_rest[1][:], in_=x_rows[:, :, x_bytes(2)].bitcast(I32))
+
+        x_codes = {}
+        x_plane = {}
+
+        def sort_x(grp, g):
+            if grp == 0:
+                raw_words = x_first[g][:]
+                raw_scales = xs_first[:, g, :]
+            else:
+                raw_words = x_rest[grp - 1][:, g, :]
+                raw_scales = xs_rest[:, g, (grp - 1) * K_PASS : grp * K_PASS]
+            plane = sbuf("x_plane%d_%d" % (grp, g), [P, PACK, P], U8)
+            codes = sbuf("x_codes%d_%d" % (grp, g), [P, PACK, P], I32)
+            nc.vector.tensor_copy(out=plane[:], in_=raw_scales.rearrange("p (m t) -> p t m", t=PACK))
+            nc.vector.tensor_copy(
+                out=codes[:].rearrange("p t m -> p m t"), in_=raw_words.rearrange("p (m t) -> p m t", t=PACK)
+            )
+            x_codes[grp, g] = codes
+            x_plane[grp, g] = plane
+
+        def interleave(copy, grouped, rows, cols):
+            copy(
+                out=grouped[:, cols, :].rearrange("p (c i) t -> p c t i", i=RUN),
+                in_=rows[:, :, cols].rearrange("p t (c i) -> p c t i", i=RUN),
+            )
+
+        psi_grouped = [sbuf("psi_grouped%d" % g, [P, MODES, PACK], BF16) for g in range(PASSES)]
+        psi_codes = [sbuf("psi_codes%d" % g, [P, MODES], I32) for g in range(PASSES)]
+        psi_plane = [sbuf("psi_plane%d" % g, [P, MODES], U8) for g in range(PASSES)]
+
+        def quantize_psi(g):
+            nc.vector.quantize_mx(
+                out=psi_codes[g][:].bitcast(FP8X4),
+                scales=psi_plane[g][:],
+                in_=psi_grouped[g][:].rearrange("p f t -> p (f t)"),
+            )
+
+        def moving(kind, g, cols):
+            if kind == "A":
+                return psi_codes[g][:, cols].bitcast(FP8X4), psi_plane[g][:, cols]
+            if kind == "E":
+                return c_codes[:, g, cols].bitcast(FP8X4), c_plane[:, g, cols]
+            words = w_first[:] if g == 0 else w_rest[:, g - 1, :]
+            return words.bitcast(FP4X4), w_plane[:, g, cols]
+
+        def product(kind, grp, first_bank, cols, pass_major):
+            width = cols.stop - cols.start
+            sums = []
+            for t in range(PACK):
+                bank = psum.tile([P, MODES], F32, name="bank%d" % (first_bank + t), tag="bank%d" % (first_bank + t))
+                sums.append(bank[:, 0:width])
+            if pass_major:
+                order = [(t, g) for g in range(PASSES) for t in range(PACK)]
+            else:
+                order = [(t, g) for t in range(PACK) for g in range(PASSES)]
+            for t, g in order:
+                rhs, rhs_scale = moving(kind, g, cols)
+                nc.tensor.matmul_mx(
+                    out=sums[t],
+                    lhsT=x_codes[grp, g][:, t, :].bitcast(FP8X4),
+                    lhsT_scale=x_plane[grp, g][:, t, :],
+                    rhs=rhs,
+                    rhs_scale=rhs_scale,
+                    start=(g == 0),
+                    stop=(g == PASSES - 1),
+                )
+            return sums
+
+        def reciprocals(b_sums):
+            inverses = []
+            for t in range(PACK):
+                root = sbuf("root", [P, MODES], F32, bufs=2)
+                inverse = sbuf("inverse", [P, MODES], F32, bufs=8)
+                nc.scalar.activation(out=root[:], in_=b_sums[t], func=ACT.Abs_reciprocal_sqrt)
+                nc.scalar.activation(out=inverse[:], in_=root[:], func=ACT.Square)
+                inverses.append(inverse)
+            return inverses
+
+        def mean_term(grp, t, e_sums, inverses):
+            mean = sbuf("mean", [P, MODES], F32, bufs=8)
+            nc.vector.scalar_tensor_tensor(
+                out=mean[:], in0=e_sums[t], scalar=h_col[:, grp, t : t + 1], in1=inverses[t][:],
+                op0=ALU.mult, op1=ALU.mult,
+            )
+            return mean
+
+        rh = sbuf("rh", [P, GROUPS, PACK], F32)
+
+        def finish(grp, t, a_sums, means, y, cols):
+            nc.vector.scalar_tensor_tensor(
+                out=y[:, t, :], in0=a_sums[t], scalar=rh[:, grp, t : t + 1], in1=means[t][:, cols],
+                op0=ALU.mult, op1=ALU.add,
+            )
+
+        def store_y(queue, grp, y, slots, cols):
+            rows = out_0[grp * K_PASS : (grp + 1) * K_PASS, :].rearrange("(p t) m -> p t m", t=PACK)
+            queue.dma_start(out=rows[:, slots, cols], in_=y[:, slots, :])
+
+        y_codes = [sbuf("y_codes%d" % grp, [P, MODES], I32) for grp in range(GROUPS)]
+        y_plane = [sbuf("y_plane%d" % grp, [P, MODES], U8) for grp in range(GROUPS)]
+
+        def quantize_y(grp, grouped, cols):
+            nc.vector.quantize_mx(
+                out=y_codes[grp][:, cols].bitcast(FP8X4),
+                scales=y_plane[grp][:, cols],
+                in_=grouped[:].rearrange("p f t -> p (f t)"),
+            )
+
+        def store_words(queue, grp, cols):
+            words = out_1[grp].rearrange("p m t -> p (m t)").bitcast(I32)
+            queue.dma_start(out=words[:, cols], in_=y_codes[grp][:, cols])
+
+        def store_scales(queue, grp, quad):
+            queue.dma_start(
+                out=out_2[grp, 4 * quad : 4 * quad + 4, :].bitcast(I32),
+                in_=y_plane[grp][live_rows(quad), :].bitcast(I32),
+            )
+
+        low, high = 0, PACK
+
+        def new_y(grp):
+            y = sbuf("y%d" % grp, [P, PACK, MODES], F32)
+            grouped = sbuf("y_grouped%d" % grp, [P, MODES, PACK], BF16)
+            return y, grouped
+
+        def finish_and_store(grp, t, a_sums, means, y, cols):
+            finish(grp, t, a_sums, means, y, cols)
+            if t % 2 == 1:
+                store_y(nc.sync, grp, y, slice(t - 1, t + 1), cols)
+
+        def hand_out(grp, grouped):
+            quantize_y(grp, grouped, all_modes)
+            store_words(nc.sync, grp, all_modes)
+            for quad in range(QUADS):
+                store_scales(nc.sync, grp, quad)
+
+        for g in range(PASSES):
+            sort_x(0, g)
+        b_sums = product("B", 0, low, all_modes, True)
+        inverses0 = reciprocals(b_sums)
+        interleave(nc.vector.tensor_copy, psi_grouped[0], psi_raw[0], all_modes)
+        sort_x(1, 0)
+        quantize_psi(0)
+        sort_x(1, 1)
+        sort_x(1, 2)
+        e_sums0 = product("E", 0, high, all_modes, False)
+        means0 = [mean_term(0, 0, e_sums0, inverses0)]
+        interleave(nc.vector.tensor_copy, psi_grouped[1], psi_raw[1], all_modes)
+        means0.append(mean_term(0, 1, e_sums0, inverses0))
+        quantize_psi(1)
+        means0.append(mean_term(0, 2, e_sums0, inverses0))
+        interleave(nc.vector.tensor_copy, psi_grouped[2], psi_raw[2], all_modes)
+        means0.append(mean_term(0, 3, e_sums0, inverses0))
+        quantize_psi(2)
+        nc.vector.tensor_tensor(out=rh[:], in0=r_col[:], in1=h_col[:], op=ALU.mult)
+
+        b_sums = product("B", 1, low, all_modes, False)
+        inverses1 = reciprocals(b_sums)
+        e_sums1 = product("E", 1, high, all_modes, False)
+        means1 = [mean_term(1, 0, e_sums1, inverses1)]
+        for g in range(PASSES):
+            sort_x(2, g)
+
+        a_sums = product("A", 0, low, all_modes, False)
+        y0, grouped0 = new_y(0)
+        for t in range(PACK):
+            if t + 1 < PACK:
+                means1.append(mean_term(1, t + 1, e_sums1, inverses1))
+            finish_and_store(0, t, a_sums, means0, y0, all_modes)
+        interleave(nc.vector.tensor_copy, grouped0, y0, all_modes)
+
+        b_sums = product("B", 2, high, all_modes, False)
+        inverses2 = reciprocals(b_sums)
+        a_sums = product("A", 1, low, all_modes, False)
+        y1, grouped1 = new_y(1)
+        finish_and_store(1, 0, a_sums, means1, y1, all_modes)
+        hand_out(0, grouped0)
+        for t in range(1, PACK):
+            finish_and_store(1, t, a_sums, means1, y1, all_modes)
+        interleave(nc.scalar.copy, grouped1, y1, all_modes)
+
+        e_sums2 = product("E", 2, high, all_modes, False)
+        means2 = [mean_term(2, t, e_sums2, inverses2) for t in range(PACK - 1)]
+        hand_out(1, grouped1)
+        means2.append(mean_term(2, PACK - 1, e_sums2, inverses2))
+
+        halves = [slice(0, HALF), slice(HALF, MODES)]
+        local = slice(0, HALF)
+        y_half = [sbuf("y_half%d" % i, [P, PACK, HALF], F32) for i in range(2)]
+        grouped_half = [sbuf("y_grouped_half%d" % i, [P, HALF, PACK], BF16) for i in range(2)]
+        a_sums = product("A", 2, low, halves[0], False)
+        for t in range(PACK):
+            finish(2, t, a_sums, means2, y_half[0], halves[0])
+        store_y(nc.sync, 2, y_half[0], slice(0, PACK), halves[0])
+        interleave(nc.scalar.copy, grouped_half[0], y_half[0], local)
+        a_sums = product("A", 2, high, halves[1], False)
+        for t in range(PACK):
+            finish_and_store(2, t, a_sums, means2, y_half[1], halves[1])
+        interleave(nc.vector.tensor_copy, grouped_half[1], y_half[1], local)
+        quantize_y(2, grouped_half[0], halves[0])
+        store_words(nc.scalar, 2, halves[0])
+        quantize_y(2, grouped_half[1], halves[1])
+        store_words(nc.sync, 2, halves[1])
+        for quad in range(QUADS):
+            store_scales(nc.scalar if quad % 2 == 0 else nc.sync, 2, quad)

@@ -47,68 +47,65 @@ def tile_diffusion_map_step_k3_kernel(
         w_rows = w_words.rearrange("g p b -> p g b")
         c_rows = c_words.rearrange("g p n t -> p g (n t)")
 
-        xs_first = sbuf("xs_first", [P, PASSES, K_PASS], U8)
-        xs_rest = sbuf("xs_rest", [P, PASSES, 2 * K_PASS], U8)
+        xs_raw = [sbuf("xs_raw%d" % grp, [P, PASSES, K_PASS], U8) for grp in range(GROUPS)]
         w_plane = sbuf("w_plane", [P, PASSES, MODES], U8)
         c_plane = sbuf("c_plane", [P, PASSES, MODES], U8)
-        for plane in (xs_first, w_plane, c_plane, xs_rest):
+        for plane in (xs_raw[0], w_plane, c_plane, xs_raw[1], xs_raw[2]):
             nc.vector.memset(plane[:].bitcast(I32), 0)
 
-        x_first = [sbuf("x_first%d" % g, [P, K_PASS], I32) for g in range(PASSES)]
-        x_rest = [sbuf("x_rest%d" % i, [P, PASSES, K_PASS], I32) for i in range(GROUPS - 1)]
+        x_raw = {
+            (grp, g): sbuf("x_raw%d_%d" % (grp, g), [P, K_PASS], I32) for grp in range(GROUPS) for g in range(PASSES)
+        }
         w_first = sbuf("w_first", [P, 2 * MODES], U8)
         w_rest = sbuf("w_rest", [P, PASSES - 1, 2 * MODES], U8)
         c_codes = sbuf("c_codes", [P, PASSES, MODES], I32)
         psi_raw = [sbuf("psi_raw%d" % g, [P, PACK, MODES], BF16) for g in range(PASSES)]
         r_col = sbuf("r_col", [P, GROUPS, PACK], BF16)
         h_col = sbuf("h_col", [P, GROUPS, PACK], BF16)
-
-        def x_bytes(grp):
-            return slice(grp * K_PASS * PACK, (grp + 1) * K_PASS * PACK)
-
-        first_cols = slice(0, K_PASS)
         all_modes = slice(0, MODES)
-        load_scales(nc.sync, xs_first, x_scales, first_cols, 0)
-        load_scales(nc.scalar, w_plane, w_scales, all_modes, 0)
-        nc.sync.dma_start(out=x_first[0][:], in_=x_rows[:, 0, x_bytes(0)].bitcast(I32))
-        nc.scalar.dma_start(out=w_first[:].bitcast(I32), in_=w_rows[:, 0, :].bitcast(I32))
-        load_scales(nc.sync, xs_first, x_scales, first_cols, 1)
-        load_scales(nc.scalar, w_plane, w_scales, all_modes, 1)
-        load_scales(nc.sync, xs_first, x_scales, first_cols, 2)
-        load_scales(nc.scalar, xs_first, x_scales, first_cols, 3)
-        load_scales(nc.sync, w_plane, w_scales, all_modes, 2)
-        load_scales(nc.scalar, w_plane, w_scales, all_modes, 3)
-        nc.sync.dma_start(out=x_first[1][:], in_=x_rows[:, 1, x_bytes(0)].bitcast(I32))
-        nc.sync.dma_start(out=w_rest[:].bitcast(I32), in_=w_rows[:, 1:, :].bitcast(I32))
-        nc.sync.dma_start(out=x_first[2][:], in_=x_rows[:, 2, x_bytes(0)].bitcast(I32))
-        for quad in range(QUADS):
-            load_scales(nc.sync, c_plane, c_scales, all_modes, quad)
-        nc.sync.dma_start(out=c_codes[:], in_=c_rows.bitcast(I32))
+
+        def load_x(grp, g):
+            span = slice(grp * K_PASS * PACK, (grp + 1) * K_PASS * PACK)
+            nc.sync.dma_start(out=x_raw[grp, g][:], in_=x_rows[:, g, span].bitcast(I32))
+
+        def load_x_scales(queue, grp, quad):
+            load_scales(queue, xs_raw[grp], x_scales, slice(grp * K_PASS, (grp + 1) * K_PASS), quad)
 
         def load_psi(g):
             rows = psi_h[g * K_PASS : (g + 1) * K_PASS, :]
             nc.sync.dma_start(out=psi_raw[g][:], in_=rows.rearrange("(p j) f -> p j f", j=PACK))
 
-        load_psi(0)
+        load_x(0, 0)
+        nc.scalar.dma_start(out=w_first[:].bitcast(I32), in_=w_rows[:, 0, :].bitcast(I32))
         for quad in range(QUADS):
-            load_scales(nc.sync, xs_rest, x_scales, slice(K_PASS, CELLS), quad)
-        nc.sync.dma_start(out=x_rest[0][:], in_=x_rows[:, :, x_bytes(1)].bitcast(I32))
+            load_x_scales(nc.sync if quad % 2 == 0 else nc.scalar, 0, quad)
+        for quad in range(QUADS):
+            load_scales(nc.sync if quad % 2 == 0 else nc.scalar, w_plane, w_scales, all_modes, quad)
+        load_x(0, 1)
+        nc.sync.dma_start(out=w_rest[:].bitcast(I32), in_=w_rows[:, 1:, :].bitcast(I32))
+        load_x(0, 2)
+        for quad in range(QUADS):
+            load_scales(nc.sync, c_plane, c_scales, all_modes, quad)
+        nc.sync.dma_start(out=c_codes[:], in_=c_rows.bitcast(I32))
+        for quad in range(QUADS):
+            load_x_scales(nc.sync, 1, quad)
+        for g in range(PASSES):
+            load_x(1, g)
         nc.sync.dma_start(out=h_col[:], in_=h.rearrange("(g p t) -> p g t", p=P, t=PACK))
         nc.sync.dma_start(out=r_col[:], in_=r.rearrange("(g p t) -> p g t", p=P, t=PACK))
-        load_psi(1)
-        load_psi(2)
-        nc.sync.dma_start(out=x_rest[1][:], in_=x_rows[:, :, x_bytes(2)].bitcast(I32))
+        for g in range(PASSES):
+            load_psi(g)
+        for quad in range(QUADS):
+            load_x_scales(nc.sync, 2, quad)
+        for g in range(PASSES):
+            load_x(2, g)
 
         x_codes = {}
         x_plane = {}
 
         def sort_x(grp, g):
-            if grp == 0:
-                raw_words = x_first[g][:]
-                raw_scales = xs_first[:, g, :]
-            else:
-                raw_words = x_rest[grp - 1][:, g, :]
-                raw_scales = xs_rest[:, g, (grp - 1) * K_PASS : grp * K_PASS]
+            raw_words = x_raw[grp, g][:]
+            raw_scales = xs_raw[grp][:, g, :]
             plane = sbuf("x_plane%d_%d" % (grp, g), [P, PACK, P], U8)
             codes = sbuf("x_codes%d_%d" % (grp, g), [P, PACK, P], I32)
             nc.vector.tensor_copy(out=plane[:], in_=raw_scales.rearrange("p (m t) -> p t m", t=PACK))
@@ -166,14 +163,18 @@ def tile_diffusion_map_step_k3_kernel(
                 )
             return sums
 
-        def reciprocals(b_sums):
-            inverses = []
-            for t in range(PACK):
-                root = sbuf("root", [P, MODES], F32, bufs=2)
-                inverse = sbuf("inverse", [P, MODES], F32, bufs=8)
-                nc.scalar.activation(out=root[:], in_=b_sums[t], func=ACT.Abs_reciprocal_sqrt)
-                nc.scalar.activation(out=inverse[:], in_=root[:], func=ACT.Square)
-                inverses.append(inverse)
+        def reciprocals(b_sums, banks_first):
+            roots = [sbuf("root", [P, MODES], F32, bufs=PACK) for t in range(PACK)]
+            inverses = [sbuf("inverse", [P, MODES], F32, bufs=2 * PACK) for t in range(PACK)]
+            if banks_first:
+                order = [(step, t) for step in range(2) for t in range(PACK)]
+            else:
+                order = [(step, t) for t in range(PACK) for step in range(2)]
+            for step, t in order:
+                if step == 0:
+                    nc.scalar.activation(out=roots[t][:], in_=b_sums[t], func=ACT.Abs_reciprocal_sqrt)
+                else:
+                    nc.scalar.activation(out=inverses[t][:], in_=roots[t][:], func=ACT.Square)
             return inverses
 
         def mean_term(grp, t, e_sums, inverses):
@@ -237,40 +238,37 @@ def tile_diffusion_map_step_k3_kernel(
         for g in range(PASSES):
             sort_x(0, g)
         b_sums = product("B", 0, low, all_modes, True)
-        inverses0 = reciprocals(b_sums)
-        interleave(nc.vector.tensor_copy, psi_grouped[0], psi_raw[0], all_modes)
-        sort_x(1, 0)
-        quantize_psi(0)
-        sort_x(1, 1)
-        sort_x(1, 2)
+        inverses0 = reciprocals(b_sums, False)
+        interleave(nc.scalar.copy, psi_grouped[0], psi_raw[0], all_modes)
+        for g in range(PASSES):
+            sort_x(1, g)
         e_sums0 = product("E", 0, high, all_modes, False)
         means0 = [mean_term(0, 0, e_sums0, inverses0)]
-        interleave(nc.vector.tensor_copy, psi_grouped[1], psi_raw[1], all_modes)
         means0.append(mean_term(0, 1, e_sums0, inverses0))
-        quantize_psi(1)
+        interleave(nc.vector.tensor_copy, psi_grouped[1], psi_raw[1], all_modes)
         means0.append(mean_term(0, 2, e_sums0, inverses0))
-        interleave(nc.vector.tensor_copy, psi_grouped[2], psi_raw[2], all_modes)
+        quantize_psi(1)
         means0.append(mean_term(0, 3, e_sums0, inverses0))
-        quantize_psi(2)
+        interleave(nc.vector.tensor_copy, psi_grouped[2], psi_raw[2], all_modes)
+        quantize_psi(0)
         nc.vector.tensor_tensor(out=rh[:], in0=r_col[:], in1=h_col[:], op=ALU.mult)
+        quantize_psi(2)
 
-        b_sums = product("B", 1, low, all_modes, False)
-        inverses1 = reciprocals(b_sums)
+        b_sums = product("B", 1, low, all_modes, True)
+        inverses1 = reciprocals(b_sums, True)
         e_sums1 = product("E", 1, high, all_modes, False)
-        means1 = [mean_term(1, 0, e_sums1, inverses1)]
         for g in range(PASSES):
             sort_x(2, g)
+        means1 = [mean_term(1, t, e_sums1, inverses1) for t in range(PACK)]
 
         a_sums = product("A", 0, low, all_modes, False)
         y0, grouped0 = new_y(0)
         for t in range(PACK):
-            if t + 1 < PACK:
-                means1.append(mean_term(1, t + 1, e_sums1, inverses1))
             finish_and_store(0, t, a_sums, means0, y0, all_modes)
         interleave(nc.vector.tensor_copy, grouped0, y0, all_modes)
 
         b_sums = product("B", 2, high, all_modes, False)
-        inverses2 = reciprocals(b_sums)
+        inverses2 = reciprocals(b_sums, False)
         a_sums = product("A", 1, low, all_modes, False)
         y1, grouped1 = new_y(1)
         finish_and_store(1, 0, a_sums, means1, y1, all_modes)

@@ -40,8 +40,8 @@ def tile_diffusion_map_step_k3_kernel(
             return slice(32 * quad, 32 * quad + 4)
 
         def load_scales(queue, plane, scales, cols, quad):
-            rows = scales[:, 4 * quad : 4 * quad + 4, cols].rearrange("g r n -> r g n")
-            queue.dma_start(out=plane[live_rows(quad), :, :].bitcast(I32), in_=rows.bitcast(I32))
+            rows = scales[:, :, cols].rearrange("g (q r) n -> r q g n", r=4)[quad]
+            queue.dma_start(out=plane[quad:P:32, :, :].bitcast(I32), in_=rows.bitcast(I32))
 
         x_rows = x_words.rearrange("g p n t -> p g (n t)")
         w_rows = w_words.rearrange("g p b -> p g b")
@@ -50,15 +50,19 @@ def tile_diffusion_map_step_k3_kernel(
         xs_raw = [sbuf("xs_raw%d" % grp, [P, PASSES, K_PASS], U8) for grp in range(GROUPS)]
         w_plane = sbuf("w_plane", [P, PASSES, MODES], U8)
         c_plane = sbuf("c_plane", [P, PASSES, MODES], U8)
-        for plane in (xs_raw[0], w_plane, c_plane, xs_raw[1], xs_raw[2]):
+        for plane in (xs_raw[0], w_plane, xs_raw[1], xs_raw[2], c_plane):
             nc.vector.memset(plane[:].bitcast(I32), 0)
 
         x_raw = {
-            (grp, g): sbuf("x_raw%d_%d" % (grp, g), [P, K_PASS], I32) for grp in range(GROUPS) for g in range(PASSES)
+            (grp, g): sbuf("x_raw%d_%d" % (grp, g), [P, K_PASS], I32)
+            for grp in range(GROUPS)
+            for g in range(PASSES)
+            if grp > 0 or g == 0
         }
+        x_pair = sbuf("x_pair", [P, PASSES - 1, K_PASS], I32)
         w_first = sbuf("w_first", [P, 2 * MODES], U8)
         w_rest = sbuf("w_rest", [P, PASSES - 1, 2 * MODES], U8)
-        c_codes = sbuf("c_codes", [P, PASSES, MODES], I32)
+        c_codes = [sbuf("c_codes%d" % g, [P, MODES], I32) for g in range(PASSES)]
         psi_raw = [sbuf("psi_raw%d" % g, [P, PACK, MODES], BF16) for g in range(PASSES)]
         r_col = sbuf("r_col", [P, GROUPS, PACK], BF16)
         h_col = sbuf("h_col", [P, GROUPS, PACK], BF16)
@@ -75,45 +79,53 @@ def tile_diffusion_map_step_k3_kernel(
             rows = psi_h[g * K_PASS : (g + 1) * K_PASS, :]
             nc.sync.dma_start(out=psi_raw[g][:], in_=rows.rearrange("(p j) f -> p j f", j=PACK))
 
+        def load_c(g):
+            nc.sync.dma_start(out=c_codes[g][:], in_=c_rows[:, g, :].bitcast(I32))
+
         load_x(0, 0)
-        nc.scalar.dma_start(out=w_first[:].bitcast(I32), in_=w_rows[:, 0, :].bitcast(I32))
         for quad in range(QUADS):
-            load_x_scales(nc.sync if quad % 2 == 0 else nc.scalar, 0, quad)
+            load_x_scales(nc.sync, 0, quad)
+        nc.sync.dma_start(out=w_first[:].bitcast(I32), in_=w_rows[:, 0, :].bitcast(I32))
+        nc.sync.dma_start(out=x_pair[:], in_=x_rows[:, 1:, 0 : K_PASS * PACK].bitcast(I32))
         for quad in range(QUADS):
-            load_scales(nc.sync if quad % 2 == 0 else nc.scalar, w_plane, w_scales, all_modes, quad)
-        load_x(0, 1)
+            load_scales(nc.sync, w_plane, w_scales, all_modes, quad)
         nc.sync.dma_start(out=w_rest[:].bitcast(I32), in_=w_rows[:, 1:, :].bitcast(I32))
-        load_x(0, 2)
+        for grp in range(1, GROUPS):
+            for quad in range(QUADS):
+                if quad < PASSES:
+                    load_x(grp, quad)
+                load_x_scales(nc.sync, grp, quad)
         for quad in range(QUADS):
+            if quad < 2:
+                load_psi(quad)
             load_scales(nc.sync, c_plane, c_scales, all_modes, quad)
-        nc.sync.dma_start(out=c_codes[:], in_=c_rows.bitcast(I32))
-        for quad in range(QUADS):
-            load_x_scales(nc.sync, 1, quad)
         for g in range(PASSES):
-            load_x(1, g)
+            load_c(g)
         nc.sync.dma_start(out=h_col[:], in_=h.rearrange("(g p t) -> p g t", p=P, t=PACK))
+        load_psi(2)
         nc.sync.dma_start(out=r_col[:], in_=r.rearrange("(g p t) -> p g t", p=P, t=PACK))
-        for g in range(PASSES):
-            load_psi(g)
-        for quad in range(QUADS):
-            load_x_scales(nc.sync, 2, quad)
-        for g in range(PASSES):
-            load_x(2, g)
 
         x_codes = {}
         x_plane = {}
 
-        def sort_x(grp, g):
-            raw_words = x_raw[grp, g][:]
-            raw_scales = xs_raw[grp][:, g, :]
-            plane = sbuf("x_plane%d_%d" % (grp, g), [P, PACK, P], U8)
+        def sort_words(grp, g):
+            raw_words = x_raw[grp, g][:] if (grp, g) in x_raw else x_pair[:, g - 1, :]
             codes = sbuf("x_codes%d_%d" % (grp, g), [P, PACK, P], I32)
-            nc.vector.tensor_copy(out=plane[:], in_=raw_scales.rearrange("p (m t) -> p t m", t=PACK))
             nc.vector.tensor_copy(
                 out=codes[:].rearrange("p t m -> p m t"), in_=raw_words.rearrange("p (m t) -> p m t", t=PACK)
             )
             x_codes[grp, g] = codes
+
+        def sort_scales(grp, g):
+            plane = sbuf("x_plane%d_%d" % (grp, g), [P, PACK, P], U8)
+            nc.vector.tensor_copy(out=plane[:], in_=xs_raw[grp][:, g, :].rearrange("p (m t) -> p t m", t=PACK))
             x_plane[grp, g] = plane
+
+        def sort_group(grp):
+            for g in range(PASSES):
+                sort_words(grp, g)
+            for g in range(PASSES):
+                sort_scales(grp, g)
 
         def interleave(copy, grouped, rows, cols):
             copy(
@@ -136,7 +148,7 @@ def tile_diffusion_map_step_k3_kernel(
             if kind == "A":
                 return psi_codes[g][:, cols].bitcast(FP8X4), psi_plane[g][:, cols]
             if kind == "E":
-                return c_codes[:, g, cols].bitcast(FP8X4), c_plane[:, g, cols]
+                return c_codes[g][:, cols].bitcast(FP8X4), c_plane[:, g, cols]
             words = w_first[:] if g == 0 else w_rest[:, g - 1, :]
             return words.bitcast(FP4X4), w_plane[:, g, cols]
 
@@ -163,33 +175,29 @@ def tile_diffusion_map_step_k3_kernel(
                 )
             return sums
 
-        def reciprocals(b_sums, banks_first):
+        def reciprocals(b_sums):
             roots = [sbuf("root", [P, MODES], F32, bufs=PACK) for t in range(PACK)]
-            inverses = [sbuf("inverse", [P, MODES], F32, bufs=2 * PACK) for t in range(PACK)]
-            if banks_first:
-                order = [(step, t) for step in range(2) for t in range(PACK)]
-            else:
-                order = [(step, t) for t in range(PACK) for step in range(2)]
-            for step, t in order:
-                if step == 0:
+            inverses = [sbuf("inverse", [P, MODES], F32, bufs=GROUPS * PACK) for t in range(PACK)]
+            for t in range(PACK + 1):
+                if t < PACK:
                     nc.scalar.activation(out=roots[t][:], in_=b_sums[t], func=ACT.Abs_reciprocal_sqrt)
-                else:
-                    nc.scalar.activation(out=inverses[t][:], in_=roots[t][:], func=ACT.Square)
+                if t > 0:
+                    nc.scalar.activation(out=inverses[t - 1][:], in_=roots[t - 1][:], func=ACT.Square)
             return inverses
 
-        def mean_term(grp, t, e_sums, inverses):
-            mean = sbuf("mean", [P, MODES], F32, bufs=8)
+        def mean_term(grp, t, e_sums, inverses, cols):
+            mean = sbuf("mean", [P, cols.stop - cols.start], F32, bufs=8)
             nc.vector.scalar_tensor_tensor(
-                out=mean[:], in0=e_sums[t], scalar=h_col[:, grp, t : t + 1], in1=inverses[t][:],
+                out=mean[:], in0=e_sums[t], scalar=h_col[:, grp, t : t + 1], in1=inverses[t][:, cols],
                 op0=ALU.mult, op1=ALU.mult,
             )
             return mean
 
         rh = sbuf("rh", [P, GROUPS, PACK], F32)
 
-        def finish(grp, t, a_sums, means, y, cols):
+        def finish(grp, t, a_sum, mean, y):
             nc.vector.scalar_tensor_tensor(
-                out=y[:, t, :], in0=a_sums[t], scalar=rh[:, grp, t : t + 1], in1=means[t][:, cols],
+                out=y, in0=a_sum, scalar=rh[:, grp, t : t + 1], in1=mean,
                 op0=ALU.mult, op1=ALU.add,
             )
 
@@ -204,7 +212,7 @@ def tile_diffusion_map_step_k3_kernel(
             nc.vector.quantize_mx(
                 out=y_codes[grp][:, cols].bitcast(FP8X4),
                 scales=y_plane[grp][:, cols],
-                in_=grouped[:].rearrange("p f t -> p (f t)"),
+                in_=grouped.rearrange("p f t -> p (f t)"),
             )
 
         def store_words(queue, grp, cols):
@@ -219,85 +227,86 @@ def tile_diffusion_map_step_k3_kernel(
 
         low, high = 0, PACK
 
-        def new_y(grp):
-            y = sbuf("y%d" % grp, [P, PACK, MODES], F32)
-            grouped = sbuf("y_grouped%d" % grp, [P, MODES, PACK], BF16)
-            return y, grouped
-
-        def finish_and_store(grp, t, a_sums, means, y, cols):
-            finish(grp, t, a_sums, means, y, cols)
-            if t % 2 == 1:
-                store_y(nc.sync, grp, y, slice(t - 1, t + 1), cols)
-
-        def hand_out(grp, grouped):
-            quantize_y(grp, grouped, all_modes)
-            store_words(nc.sync, grp, all_modes)
-            for quad in range(QUADS):
-                store_scales(nc.sync, grp, quad)
-
-        for g in range(PASSES):
-            sort_x(0, g)
-        b_sums = product("B", 0, low, all_modes, True)
-        inverses0 = reciprocals(b_sums, False)
-        interleave(nc.scalar.copy, psi_grouped[0], psi_raw[0], all_modes)
-        for g in range(PASSES):
-            sort_x(1, g)
-        e_sums0 = product("E", 0, high, all_modes, False)
-        means0 = [mean_term(0, 0, e_sums0, inverses0)]
-        means0.append(mean_term(0, 1, e_sums0, inverses0))
-        interleave(nc.vector.tensor_copy, psi_grouped[1], psi_raw[1], all_modes)
-        means0.append(mean_term(0, 2, e_sums0, inverses0))
-        quantize_psi(1)
-        means0.append(mean_term(0, 3, e_sums0, inverses0))
-        interleave(nc.vector.tensor_copy, psi_grouped[2], psi_raw[2], all_modes)
-        quantize_psi(0)
-        nc.vector.tensor_tensor(out=rh[:], in0=r_col[:], in1=h_col[:], op=ALU.mult)
-        quantize_psi(2)
-
-        b_sums = product("B", 1, low, all_modes, True)
-        inverses1 = reciprocals(b_sums, True)
-        e_sums1 = product("E", 1, high, all_modes, False)
-        for g in range(PASSES):
-            sort_x(2, g)
-        means1 = [mean_term(1, t, e_sums1, inverses1) for t in range(PACK)]
-
-        a_sums = product("A", 0, low, all_modes, False)
-        y0, grouped0 = new_y(0)
-        for t in range(PACK):
-            finish_and_store(0, t, a_sums, means0, y0, all_modes)
-        interleave(nc.vector.tensor_copy, grouped0, y0, all_modes)
-
-        b_sums = product("B", 2, high, all_modes, False)
-        inverses2 = reciprocals(b_sums, False)
-        a_sums = product("A", 1, low, all_modes, False)
-        y1, grouped1 = new_y(1)
-        finish_and_store(1, 0, a_sums, means1, y1, all_modes)
-        hand_out(0, grouped0)
-        for t in range(1, PACK):
-            finish_and_store(1, t, a_sums, means1, y1, all_modes)
-        interleave(nc.scalar.copy, grouped1, y1, all_modes)
-
-        e_sums2 = product("E", 2, high, all_modes, False)
-        means2 = [mean_term(2, t, e_sums2, inverses2) for t in range(PACK - 1)]
-        hand_out(1, grouped1)
-        means2.append(mean_term(2, PACK - 1, e_sums2, inverses2))
-
         halves = [slice(0, HALF), slice(HALF, MODES)]
-        local = slice(0, HALF)
-        y_half = [sbuf("y_half%d" % i, [P, PACK, HALF], F32) for i in range(2)]
-        grouped_half = [sbuf("y_grouped_half%d" % i, [P, HALF, PACK], BF16) for i in range(2)]
-        a_sums = product("A", 2, low, halves[0], False)
-        for t in range(PACK):
-            finish(2, t, a_sums, means2, y_half[0], halves[0])
-        store_y(nc.sync, 2, y_half[0], slice(0, PACK), halves[0])
-        interleave(nc.scalar.copy, grouped_half[0], y_half[0], local)
-        a_sums = product("A", 2, high, halves[1], False)
-        for t in range(PACK):
-            finish_and_store(2, t, a_sums, means2, y_half[1], halves[1])
-        interleave(nc.vector.tensor_copy, grouped_half[1], y_half[1], local)
-        quantize_y(2, grouped_half[0], halves[0])
-        store_words(nc.scalar, 2, halves[0])
-        quantize_y(2, grouped_half[1], halves[1])
+
+        def diffuse_half(grp, half, first_bank, means, copy):
+            cols = halves[half]
+            a_sums = product("A", grp, first_bank, cols, False)
+            y = sbuf("y%d_%d" % (grp, half), [P, PACK, HALF], F32)
+            grouped = sbuf("y_grouped%d_%d" % (grp, half), [P, HALF, PACK], BF16)
+            for t in range(PACK):
+                finish(grp, t, a_sums[t], means[t], y[:, t, :])
+                if t % 2 == 1:
+                    store_y(nc.sync, grp, y, slice(t - 1, t + 1), cols)
+            interleave(copy, grouped, y, slice(0, HALF))
+            return grouped
+
+        def hand_out(grp, half, grouped):
+            quantize_y(grp, grouped[:], halves[half])
+            if half == 1:
+                store_words(nc.sync, grp, all_modes)
+                for quad in range(QUADS):
+                    store_scales(nc.sync, grp, quad)
+
+        def interleave_psi(g):
+            interleave(nc.vector.tensor_copy, psi_grouped[g], psi_raw[g], all_modes)
+
+        inverses = []
+        for grp in range(GROUPS):
+            if grp == 0:
+                for g in range(PASSES):
+                    sort_words(0, g)
+                    sort_scales(0, g)
+            else:
+                sort_group(grp)
+            inverses.append(reciprocals(product("B", grp, (low, high)[grp % 2], all_modes, True)))
+        interleave_psi(0)
+        interleave_psi(1)
+        quantize_psi(0)
+        quantize_psi(1)
+        interleave_psi(2)
+        nc.vector.tensor_tensor(out=rh[:], in0=r_col[:], in1=h_col[:], op=ALU.mult)
+
+        e_sums = product("E", 0, high, all_modes, False)
+        means0 = [mean_term(0, 0, e_sums, inverses[0], all_modes)]
+        quantize_psi(2)
+        means0.extend(mean_term(0, t, e_sums, inverses[0], all_modes) for t in range(1, PACK))
+        e_sums = product("E", 1, low, all_modes, False)
+        means1 = [mean_term(1, t, e_sums, inverses[1], all_modes) for t in range(PACK)]
+
+        grouped00 = diffuse_half(0, 0, high, [m[:, halves[0]] for m in means0], nc.scalar.copy)
+        grouped01 = diffuse_half(0, 1, low, [m[:, halves[1]] for m in means0], nc.scalar.copy)
+        grouped10 = diffuse_half(1, 0, high, [m[:, halves[0]] for m in means1], nc.scalar.copy)
+        hand_out(0, 0, grouped00)
+        grouped11 = diffuse_half(1, 1, low, [m[:, halves[1]] for m in means1], nc.scalar.copy)
+        hand_out(0, 1, grouped01)
+
+        e_sums = product("E", 2, high, halves[0], False)
+        means2 = [mean_term(2, t, e_sums, inverses[2], halves[0]) for t in range(PACK)]
+        hand_out(1, 0, grouped10)
+        grouped20 = diffuse_half(2, 0, low, [m[:] for m in means2], nc.scalar.copy)
+        hand_out(1, 1, grouped11)
+        e_sums = product("E", 2, high, halves[1], False)
+        means2 = [mean_term(2, t, e_sums, inverses[2], halves[1]) for t in range(PACK)]
+
+        a_sums = product("A", 2, low, halves[1], False)
+        y = sbuf("y_last", [P, PACK, HALF], F32)
+        grouped = sbuf("y_grouped_last", [P, HALF, PACK], BF16)
+        for t in range(PACK - 1):
+            finish(2, t, a_sums[t], means2[t][:], y[:, t, :])
+            if t == 0:
+                quantize_y(2, grouped20[:], halves[0])
+                store_words(nc.sync, 2, halves[0])
+        store_y(nc.sync, 2, y, slice(0, PACK - 1), halves[1])
+        quarters = [slice(0, HALF // 2), slice(HALF // 2, HALF)]
+        last = PACK - 1
+        for q in quarters:
+            finish(2, last, a_sums[last][:, q], means2[last][:, q], y[:, last, q])
+        store_y(nc.sync, 2, y, slice(last, PACK), halves[1])
+        for q in quarters:
+            interleave(nc.vector.tensor_copy, grouped, y, q)
+        for q in quarters:
+            quantize_y(2, grouped[:, q, :], slice(HALF + q.start, HALF + q.stop))
         store_words(nc.sync, 2, halves[1])
         for quad in range(QUADS):
-            store_scales(nc.scalar if quad % 2 == 0 else nc.sync, 2, quad)
+            store_scales(nc.sync, 2, quad)

from contextlib import ExitStack

import concourse.mybir as mybir

CELLS, MODES = 1536, 512
FLOPS = 3 * 2 * CELLS * CELLS * MODES

F32 = mybir.dt.float32
BF16 = mybir.dt.bfloat16
I32 = mybir.dt.int32
U8 = mybir.dt.uint8
FP8X4 = mybir.dt.float8_e4m3fn_x4
FP4X4 = mybir.dt.float4_e2m1fn_x4
ALU = mybir.AluOpType
ACT = mybir.ActivationFunctionType

P = 128
PACK = 4
K_PASS = P * PACK
PASSES = CELLS // K_PASS
GROUPS = CELLS // K_PASS
QUADS = 4
RUN = 4
HALF = MODES // 2


def tile_diffusion_map_step_k3_kernel(
    tc, x_words, x_scales, psi_h, w_words, w_scales, c_words, c_scales, r, h, out_0, out_1, out_2
):
    nc = tc.nc
    with ExitStack() as ctx:
        keep = ctx.enter_context(tc.tile_pool(name="keep", bufs=1))
        psum = ctx.enter_context(tc.psum_pool(name="psum", bufs=1))
        ctx.enter_context(tc.manual_schedule())

        def sbuf(name, shape, dtype, tag="", bufs=None):
            return keep.tile(shape, dtype, name=name, tag=tag or name, bufs=bufs, align_bytes=256)

        def live_rows(quad):
            return slice(32 * quad, 32 * quad + 4)

        def load_scales(queue, plane, scales, cols, quad):
            rows = scales[:, :, cols].rearrange("g (q r) n -> r q g n", r=4)[quad]
            queue.dma_start(out=plane[quad:P:32, :, :].bitcast(I32), in_=rows.bitcast(I32))

        x_rows = x_words.rearrange("g p n t -> p g (n t)")
        w_rows = w_words.rearrange("g p b -> p g b")
        c_rows = c_words.rearrange("g p n t -> p g (n t)")

        xs_raw = [sbuf("xs_raw%d" % grp, [P, PASSES, K_PASS], U8) for grp in range(GROUPS)]
        w_plane = sbuf("w_plane", [P, PASSES, MODES], U8)
        c_plane = sbuf("c_plane", [P, PASSES, MODES], U8)
        for plane in (xs_raw[0], w_plane, xs_raw[1], xs_raw[2], c_plane):
            nc.vector.memset(plane[:].bitcast(I32), 0)

        x_raw = {
            (grp, g): sbuf("x_raw%d_%d" % (grp, g), [P, K_PASS], I32)
            for grp in range(GROUPS)
            for g in range(PASSES)
            if grp > 0 or g == 0
        }
        x_pair = sbuf("x_pair", [P, PASSES - 1, K_PASS], I32)
        w_first = sbuf("w_first", [P, 2 * MODES], U8)
        w_rest = sbuf("w_rest", [P, PASSES - 1, 2 * MODES], U8)
        c_codes = [sbuf("c_codes%d" % g, [P, MODES], I32) for g in range(PASSES)]
        psi_raw = [sbuf("psi_raw%d" % g, [P, PACK, MODES], BF16) for g in range(PASSES)]
        r_col = sbuf("r_col", [P, GROUPS, PACK], BF16)
        h_col = sbuf("h_col", [P, GROUPS, PACK], BF16)
        all_modes = slice(0, MODES)

        def load_x(grp, g):
            span = slice(grp * K_PASS * PACK, (grp + 1) * K_PASS * PACK)
            nc.sync.dma_start(out=x_raw[grp, g][:], in_=x_rows[:, g, span].bitcast(I32))

        def load_x_scales(queue, grp, quad):
            load_scales(queue, xs_raw[grp], x_scales, slice(grp * K_PASS, (grp + 1) * K_PASS), quad)

        def load_psi(g):
            rows = psi_h[g * K_PASS : (g + 1) * K_PASS, :]
            nc.sync.dma_start(out=psi_raw[g][:], in_=rows.rearrange("(p j) f -> p j f", j=PACK))

        def load_c(g):
            nc.sync.dma_start(out=c_codes[g][:], in_=c_rows[:, g, :].bitcast(I32))

        load_x(0, 0)
        for quad in range(QUADS):
            load_x_scales(nc.sync, 0, quad)
        nc.sync.dma_start(out=w_first[:].bitcast(I32), in_=w_rows[:, 0, :].bitcast(I32))
        nc.sync.dma_start(out=x_pair[:], in_=x_rows[:, 1:, 0 : K_PASS * PACK].bitcast(I32))
        for quad in range(QUADS):
            load_scales(nc.sync, w_plane, w_scales, all_modes, quad)
        nc.sync.dma_start(out=w_rest[:].bitcast(I32), in_=w_rows[:, 1:, :].bitcast(I32))
        for grp in range(1, GROUPS):
            for quad in range(QUADS):
                if quad < PASSES:
                    load_x(grp, quad)
                load_x_scales(nc.sync, grp, quad)
        for quad in range(QUADS):
            if quad < 2:
                load_psi(quad)
            load_scales(nc.sync, c_plane, c_scales, all_modes, quad)
        for g in range(PASSES):
            load_c(g)
        nc.sync.dma_start(out=h_col[:], in_=h.rearrange("(g p t) -> p g t", p=P, t=PACK))
        load_psi(2)
        nc.sync.dma_start(out=r_col[:], in_=r.rearrange("(g p t) -> p g t", p=P, t=PACK))

        x_codes = {}
        x_plane = {}

        def sort_words(grp, g):
            raw_words = x_raw[grp, g][:] if (grp, g) in x_raw else x_pair[:, g - 1, :]
            codes = sbuf("x_codes%d_%d" % (grp, g), [P, PACK, P], I32)
            nc.vector.tensor_copy(
                out=codes[:].rearrange("p t m -> p m t"), in_=raw_words.rearrange("p (m t) -> p m t", t=PACK)
            )
            x_codes[grp, g] = codes

        def sort_scales(grp, g):
            plane = sbuf("x_plane%d_%d" % (grp, g), [P, PACK, P], U8)
            nc.vector.tensor_copy(out=plane[:], in_=xs_raw[grp][:, g, :].rearrange("p (m t) -> p t m", t=PACK))
            x_plane[grp, g] = plane

        def sort_group(grp):
            for g in range(PASSES):
                sort_words(grp, g)
            for g in range(PASSES):
                sort_scales(grp, g)

        def interleave(copy, grouped, rows, cols):
            copy(
                out=grouped[:, cols, :].rearrange("p (c i) t -> p c t i", i=RUN),
                in_=rows[:, :, cols].rearrange("p t (c i) -> p c t i", i=RUN),
            )

        psi_grouped = [sbuf("psi_grouped%d" % g, [P, MODES, PACK], BF16) for g in range(PASSES)]
        psi_codes = [sbuf("psi_codes%d" % g, [P, MODES], I32) for g in range(PASSES)]
        psi_plane = [sbuf("psi_plane%d" % g, [P, MODES], U8) for g in range(PASSES)]

        def quantize_psi(g):
            nc.vector.quantize_mx(
                out=psi_codes[g][:].bitcast(FP8X4),
                scales=psi_plane[g][:],
                in_=psi_grouped[g][:].rearrange("p f t -> p (f t)"),
            )

        def moving(kind, g, cols):
            if kind == "A":
                return psi_codes[g][:, cols].bitcast(FP8X4), psi_plane[g][:, cols]
            if kind == "E":
                return c_codes[g][:, cols].bitcast(FP8X4), c_plane[:, g, cols]
            words = w_first[:] if g == 0 else w_rest[:, g - 1, :]
            return words.bitcast(FP4X4), w_plane[:, g, cols]

        def product(kind, grp, first_bank, cols, pass_major):
            width = cols.stop - cols.start
            sums = []
            for t in range(PACK):
                bank = psum.tile([P, MODES], F32, name="bank%d" % (first_bank + t), tag="bank%d" % (first_bank + t))
                sums.append(bank[:, 0:width])
            if pass_major:
                order = [(t, g) for g in range(PASSES) for t in range(PACK)]
            else:
                order = [(t, g) for t in range(PACK) for g in range(PASSES)]
            for t, g in order:
                rhs, rhs_scale = moving(kind, g, cols)
                nc.tensor.matmul_mx(
                    out=sums[t],
                    lhsT=x_codes[grp, g][:, t, :].bitcast(FP8X4),
                    lhsT_scale=x_plane[grp, g][:, t, :],
                    rhs=rhs,
                    rhs_scale=rhs_scale,
                    start=(g == 0),
                    stop=(g == PASSES - 1),
                )
            return sums

        def reciprocals(b_sums):
            roots = [sbuf("root", [P, MODES], F32, bufs=PACK) for t in range(PACK)]
            inverses = [sbuf("inverse", [P, MODES], F32, bufs=GROUPS * PACK) for t in range(PACK)]
            for t in range(PACK + 1):
                if t < PACK:
                    nc.scalar.activation(out=roots[t][:], in_=b_sums[t], func=ACT.Abs_reciprocal_sqrt)
                if t > 0:
                    nc.scalar.activation(out=inverses[t - 1][:], in_=roots[t - 1][:], func=ACT.Square)
            return inverses

        def mean_term(grp, t, e_sums, inverses, cols):
            mean = sbuf("mean", [P, cols.stop - cols.start], F32, bufs=8)
            nc.vector.scalar_tensor_tensor(
                out=mean[:], in0=e_sums[t], scalar=h_col[:, grp, t : t + 1], in1=inverses[t][:, cols],
                op0=ALU.mult, op1=ALU.mult,
            )
            return mean

        rh = sbuf("rh", [P, GROUPS, PACK], F32)

        def finish(grp, t, a_sum, mean, y):
            nc.vector.scalar_tensor_tensor(
                out=y, in0=a_sum, scalar=rh[:, grp, t : t + 1], in1=mean,
                op0=ALU.mult, op1=ALU.add,
            )

        def store_y(queue, grp, y, slots, cols):
            rows = out_0[grp * K_PASS : (grp + 1) * K_PASS, :].rearrange("(p t) m -> p t m", t=PACK)
            queue.dma_start(out=rows[:, slots, cols], in_=y[:, slots, :])

        y_codes = [sbuf("y_codes%d" % grp, [P, MODES], I32) for grp in range(GROUPS)]
        y_plane = [sbuf("y_plane%d" % grp, [P, MODES], U8) for grp in range(GROUPS)]

        def quantize_y(grp, grouped, cols):
            nc.vector.quantize_mx(
                out=y_codes[grp][:, cols].bitcast(FP8X4),
                scales=y_plane[grp][:, cols],
                in_=grouped.rearrange("p f t -> p (f t)"),
            )

        def store_words(queue, grp, cols):
            words = out_1[grp].rearrange("p m t -> p (m t)").bitcast(I32)
            queue.dma_start(out=words[:, cols], in_=y_codes[grp][:, cols])

        def store_scales(queue, grp, quad):
            queue.dma_start(
                out=out_2[grp, 4 * quad : 4 * quad + 4, :].bitcast(I32),
                in_=y_plane[grp][live_rows(quad), :].bitcast(I32),
            )

        low, high = 0, PACK

        halves = [slice(0, HALF), slice(HALF, MODES)]

        def diffuse_half(grp, half, first_bank, means, copy):
            cols = halves[half]
            a_sums = product("A", grp, first_bank, cols, False)
            y = sbuf("y%d_%d" % (grp, half), [P, PACK, HALF], F32)
            grouped = sbuf("y_grouped%d_%d" % (grp, half), [P, HALF, PACK], BF16)
            for t in range(PACK):
                finish(grp, t, a_sums[t], means[t], y[:, t, :])
                if t % 2 == 1:
                    store_y(nc.sync, grp, y, slice(t - 1, t + 1), cols)
            interleave(copy, grouped, y, slice(0, HALF))
            return grouped

        def hand_out(grp, half, grouped):
            quantize_y(grp, grouped[:], halves[half])
            if half == 1:
                store_words(nc.sync, grp, all_modes)
                for quad in range(QUADS):
                    store_scales(nc.sync, grp, quad)

        def interleave_psi(g):
            interleave(nc.vector.tensor_copy, psi_grouped[g], psi_raw[g], all_modes)

        inverses = []
        for grp in range(GROUPS):
            if grp == 0:
                for g in range(PASSES):
                    sort_words(0, g)
                    sort_scales(0, g)
            else:
                sort_group(grp)
            inverses.append(reciprocals(product("B", grp, (low, high)[grp % 2], all_modes, True)))
        interleave_psi(0)
        interleave_psi(1)
        quantize_psi(0)
        quantize_psi(1)
        interleave_psi(2)
        nc.vector.tensor_tensor(out=rh[:], in0=r_col[:], in1=h_col[:], op=ALU.mult)

        e_sums = product("E", 0, high, all_modes, False)
        means0 = [mean_term(0, 0, e_sums, inverses[0], all_modes)]
        quantize_psi(2)
        means0.extend(mean_term(0, t, e_sums, inverses[0], all_modes) for t in range(1, PACK))
        e_sums = product("E", 1, low, all_modes, False)
        means1 = [mean_term(1, t, e_sums, inverses[1], all_modes) for t in range(PACK)]

        grouped00 = diffuse_half(0, 0, high, [m[:, halves[0]] for m in means0], nc.scalar.copy)
        grouped01 = diffuse_half(0, 1, low, [m[:, halves[1]] for m in means0], nc.scalar.copy)
        grouped10 = diffuse_half(1, 0, high, [m[:, halves[0]] for m in means1], nc.scalar.copy)
        hand_out(0, 0, grouped00)
        grouped11 = diffuse_half(1, 1, low, [m[:, halves[1]] for m in means1], nc.scalar.copy)
        hand_out(0, 1, grouped01)

        e_sums = product("E", 2, high, halves[0], False)
        means2 = [mean_term(2, t, e_sums, inverses[2], halves[0]) for t in range(PACK)]
        hand_out(1, 0, grouped10)
        grouped20 = diffuse_half(2, 0, low, [m[:] for m in means2], nc.scalar.copy)
        hand_out(1, 1, grouped11)
        e_sums = product("E", 2, high, halves[1], False)
        means2 = [mean_term(2, t, e_sums, inverses[2], halves[1]) for t in range(PACK)]

        a_sums = product("A", 2, low, halves[1], False)
        y = sbuf("y_last", [P, PACK, HALF], F32)
        grouped = sbuf("y_grouped_last", [P, HALF, PACK], BF16)
        for t in range(PACK - 1):
            finish(2, t, a_sums[t], means2[t][:], y[:, t, :])
            if t == 0:
                quantize_y(2, grouped20[:], halves[0])
                store_words(nc.sync, 2, halves[0])
        store_y(nc.sync, 2, y, slice(0, PACK - 1), halves[1])
        quarters = [slice(0, HALF // 2), slice(HALF // 2, HALF)]
        last = PACK - 1
        for q in quarters:
            finish(2, last, a_sums[last][:, q], means2[last][:, q], y[:, last, q])
        store_y(nc.sync, 2, y, slice(last, PACK), halves[1])
        for q in quarters:
            interleave(nc.vector.tensor_copy, grouped, y, q)
        for q in quarters:
            quantize_y(2, grouped[:, q, :], slice(HALF + q.start, HALF + q.stop))
        store_words(nc.sync, 2, halves[1])
        for quad in range(QUADS):
            store_scales(nc.sync, 2, quad)
